import numpy as np
import ml_dtypes


def mxq(x, axis, fmt="e4m3"):
    dtype, down = {"e4m3": (ml_dtypes.float8_e4m3fn, 7), "e5m2": (ml_dtypes.float8_e5m2, 14)}[fmt]
    v = np.moveaxis(np.asarray(x, np.float32).astype(ml_dtypes.bfloat16).astype(np.float64), axis, -1)
    blocks = v.reshape(v.shape[:-1] + (-1, 32))
    amax = np.abs(blocks).max(-1, keepdims=True)
    byte = np.maximum(np.where(amax > 0, np.frexp(amax)[1] - 1 + 127, 0) - down, 1)
    scale = np.exp2(byte - 127.0)
    codes = (blocks / scale).astype(np.float32).astype(dtype).astype(np.float64)
    return np.moveaxis((codes * scale).reshape(v.shape), -1, axis)


WIDE = False


def mx_kscale(k):
    if not WIDE:
        return np.ones(k)
    levels = np.array([10, -10, 5, -5, 0])
    if k % 512:
        return np.exp2(np.random.permutation(np.resize(levels, k // 32))).repeat(32)
    a = np.empty((k // 512, 16))
    for p in range(k // 512):
        a[p, :8] = np.random.permutation(np.resize(levels, 8))
        for g in range(8):
            far = levels[np.abs(levels - a[p, g]) >= 10]
            a[p, g + 8] = far[np.random.randint(len(far))]
    return np.exp2(a.ravel()).repeat(32)


def f64(x):
    return np.asarray(x).astype(np.float64)


def striped(idx):
    return np.tile(idx.reshape(-1, 16).T, (8, 1)).astype(np.uint16)


def unstriped(offs):
    return offs[:16].T.reshape(-1).astype(np.int64)


E2M1 = np.array([0.0, 0.5, 1.0, 1.5, 2.0, 3.0, 4.0, 6.0, -0.0, -0.5, -1.0, -1.5, -2.0, -3.0, -4.0, -6.0])


def pack_weight(w, fmt):
    k, n = w.shape
    w = f64(np.asarray(w, np.float32).astype(ml_dtypes.bfloat16)).reshape(k // 32, 32, n)
    amax = np.abs(w).max(1)
    if fmt == "e4m3":
        byte = np.frexp(amax)[1] - 1 + 127 - 7
    else:
        mant, ex = np.frexp(amax / 6.0)
        byte = np.where(mant > 0.5, ex, ex - 1) + 127
    byte = np.clip(np.where(amax > 0, byte, 1), 1, 254)
    scaled = (w * np.exp2(127.0 - byte)[:, None, :]).reshape(k, n).astype(np.float32)
    by_word = np.ascontiguousarray(scaled.reshape(k // 512, 128, 4, n).transpose(0, 1, 3, 2))
    if fmt == "e4m3":
        words = by_word.astype(ml_dtypes.float8_e4m3fn).view(np.uint8)
    else:
        c = by_word.astype(ml_dtypes.float4_e2m1fn).view(np.uint8) & 0xF
        words = (c[..., 0::2] | (c[..., 1::2] << 4)).reshape(k // 512, 128, 2 * n)
    return np.ascontiguousarray(words), np.ascontiguousarray(byte.astype(np.uint8).reshape(k // 512, 16, n))


def unpack_weight(words, scales, fmt):
    g, _, n = scales.shape
    words = np.ascontiguousarray(words).reshape(g, 128, n, -1)
    if fmt == "e4m3":
        vals = words.view(ml_dtypes.float8_e4m3fn).astype(np.float64)
    else:
        nib = np.empty((g, 128, n, 4), np.uint8)
        nib[..., 0::2] = words & 0xF
        nib[..., 1::2] = words >> 4
        vals = E2M1[nib]
    vals = vals * np.repeat(np.exp2(scales.astype(np.float64) - 127.0), 8, axis=1)[..., None]
    return vals.transpose(0, 1, 3, 2).reshape(g * 512, n)


def gelu(v):
    return 0.5 * v * (1.0 + np.tanh(np.sqrt(2.0 / np.pi) * (v + 0.044715 * v**3)))


K, T, S, T2, P, H, N = 1024, 2048, 1024, 2048, 1024, 512, 384

def setup_inputs():
    n = np.random.standard_normal
    ks = mx_kscale(K)[:, None]
    u = mx_kscale(H)[:, None]
    tab_words, tab_scales = pack_weight(n((K, T)) * ks, "e4m3")
    w2_words, w2_scales = pack_weight(0.4 * n((K, H)) / np.sqrt(K) / ks, "e4m3")
    w4_words, w4_scales = pack_weight(0.6 * n((H, N)) / np.sqrt(H) / u, "e2m1")
    mix = np.random.choice([-1.0, 1.0], (H, P)) * np.random.uniform(2.0, 6.0, (H, P)) * u
    return {
        "tab_words": tab_words, "tab_scales": tab_scales,
        "offs": striped(np.random.permutation(T)[:S]),
        "offs2": striped(np.random.permutation(T2)[:S]),
        "offs3": striped(np.random.permutation(T2)[:P]),
        "w1": (1.7 * n((K, H)) / np.sqrt(K) / ks).astype(np.float32),
        "gain1": np.random.uniform(0.5, 1.0, H).astype(np.float32),
        "w2_words": w2_words, "w2_scales": w2_scales,
        "b2": (0.25 * n(H)).astype(np.float32),
        "page0": (0.8 * n((H, T2))).astype(np.float32),
        "wgs": np.exp(0.3 * n((128, S))).astype(np.float32),
        "temp": np.random.uniform(0.4, 1.6, H).astype(np.float32),
        "mix": mix.astype(np.float32),
        "w3": (np.random.uniform(-1.25, 1.25, (H, N)) / np.sqrt(H) / u).astype(np.float32),
        "gain2": np.random.uniform(1.5, 3.0, N).astype(np.float32),
        "w4_words": w4_words, "w4_scales": w4_scales,
        "prior": (0.4 * n((N, P))).astype(np.float32),
    }

def reference(tab_words, tab_scales, offs, offs2, offs3, w1, gain1, w2_words, w2_scales, b2,
              page0, wgs, temp, mix, w3, gain2, w4_words, w4_scales, prior):
    v = unpack_weight(tab_words, tab_scales, "e4m3")[:, unstriped(offs)]
    w2 = unpack_weight(w2_words, w2_scales, "e4m3")
    w4 = unpack_weight(w4_words, w4_scales, "e2m1")
    bent = np.tanh(mxq(f64(w1), 0, "e4m3").T @ v) * f64(gain1)[:, None]
    h = bent + (w2.T @ v) + f64(b2)[:, None]
    page = f64(page0).copy()
    page[:, unstriped(offs2)] = np.tile(f64(wgs), (H // 128, 1)) * h
    top = page.max(axis=1)
    a = np.exp(f64(temp)[:, None] * (page[:, unstriped(offs3)] - top[:, None]))
    x = mxq(a * f64(mix), 0, "e4m3")
    wave = np.sin(mxq(f64(w3), 0, "e4m3").T @ x) * f64(gain2)[:, None]
    out = wave + (w4.T @ x) + f64(prior)
    return out

@@ -1,0 +1,295 @@
+import math
+from contextlib import ExitStack
+
+import concourse.mybir as mybir
+
+K, T, S, T2, M, H, N = 1024, 2048, 1024, 2048, 1024, 512, 384
+FLOPS = 2 * (2 * K * H * S + 2 * H * N * M)
+
+F32 = mybir.dt.float32
+BF16 = mybir.dt.bfloat16
+I32 = mybir.dt.int32
+U32 = mybir.dt.uint32
+U16 = mybir.dt.uint16
+U8 = mybir.dt.uint8
+E4M3 = mybir.dt.float8_e4m3fn_x4
+E2M1 = mybir.dt.float4_e2m1fn_x4
+ACT = mybir.ActivationFunctionType
+ALU = mybir.AluOpType
+AXIS = mybir.AxisListType
+
+P = 128
+PACK = 4
+PASSES = K // (P * PACK)
+CHUNK = 512
+CHUNKS = S // CHUNK
+LIST_COLS = CHUNK // 16
+QUADS = 4
+OUT_TILES = N // P
+
+
+def tile_list_flux_reread_scores_kernel(
+    tc, tab_words, tab_scales, offs, offs2, offs3, w1, gain1, w2_words, w2_scales, b2,
+    page0, wgs, temp, mix, w3, gain2, w4_words, w4_scales, prior, out,
+):
+    nc = tc.nc
+    with ExitStack() as ctx:
+        keep = ctx.enter_context(tc.tile_pool(name="keep", bufs=1))
+        ring = ctx.enter_context(tc.tile_pool(name="ring", bufs=2))
+        hring = ctx.enter_context(tc.tile_pool(name="hring", bufs=4))
+        tail = ctx.enter_context(tc.tile_pool(name="tail", bufs=CHUNKS * OUT_TILES))
+        psum = ctx.enter_context(tc.psum_pool(name="psum", bufs=4))
+
+        def held(shape, dtype, name):
+            return keep.tile(shape, dtype, name=name, align_bytes=64)
+
+        def chunk_cols(c):
+            return slice(c * CHUNK, (c + 1) * CHUNK)
+
+        def list_cols(c):
+            return slice(c * LIST_COLS, (c + 1) * LIST_COLS)
+
+        idx = held([P, S // 16], U16, "idx")
+        idx2 = held([P, S // 16], U16, "idx2")
+        idx3 = held([P, M // 16], U16, "idx3")
+        tab = [held([P, T], U32, f"tab{a}") for a in range(PASSES)]
+        tab_sc = held([P, T], U8, "tab_sc")
+        w1_raw = [held([P, PACK, H], F32, f"w1_raw{a}") for a in range(PASSES)]
+        w2_raw = held([P, PASSES, H], I32, "w2_raw")
+        w2_raw_sc = held([P, H], U8, "w2_raw_sc")
+        w4_codes = held([P, 2 * N], U8, "w4_codes")
+        w4_sc = held([P, N], U8, "w4_sc")
+        page = [held([P, T2], F32, f"page{t}") for t in range(PACK)]
+        wg = held([P, PACK * S], F32, "wg")
+        mix_sb = held([P, PACK, M], F32, "mix_sb")
+        w3_raw = held([P, PACK, N], F32, "w3_raw")
+        prior_sb = held([P, OUT_TILES, M], F32, "prior_sb")
+        gain1_sb = held([P, PACK], F32, "gain1_sb")
+        b2_sb = held([P, PACK], F32, "b2_sb")
+        temp_sb = held([P, PACK], F32, "temp_sb")
+        gain2_sb = held([P, OUT_TILES], F32, "gain2_sb")
+
+        for plane in (tab_sc, w2_raw_sc, w4_sc):
+            nc.gpsimd.memset(plane[:].bitcast(I32), 0)
+
+        def load_scales(queue, plane, scales):
+            rows = 4 * scales.shape[0]
+            for q in range(QUADS):
+                queue.dma_start(
+                    out=plane[32 * q : 32 * q + rows, :].bitcast(I32),
+                    in_=scales[:, 4 * q : 4 * q + 4, :].bitcast(I32),
+                )
+
+        def load_table(a):
+            nc.sync.dma_start(
+                out=tab[a][:].bitcast(I32), in_=tab_words[a].rearrange("p t i -> p (t i)").bitcast(I32)
+            )
+
+        def load_w1(a):
+            rows = w1[a * P * PACK : (a + 1) * P * PACK, :]
+            nc.sync.dma_start(out=w1_raw[a][:], in_=rows.rearrange("(p j) c -> p j c", j=PACK))
+
+        page_rows = page0.rearrange("(p t) c -> t p c", t=PACK)
+        wgs_rows = wgs.rearrange("(q t) j -> q (t j)", t=PACK)
+
+        def load_wgs(lo, hi):
+            for q in range(QUADS):
+                nc.sync.dma_start(out=wg[32 * q : 32 * q + 32, lo:hi], in_=wgs_rows[:, lo:hi])
+
+        nc.sync.dma_start(idx[:], offs)
+        load_table(0)
+        load_scales(nc.scalar, tab_sc, tab_scales)
+        load_w1(0)
+        load_w1(1)
+        load_scales(nc.sync, w2_raw_sc, w2_scales)
+        for vec_sb, vec in ((gain1_sb, gain1), (b2_sb, b2)):
+            nc.sync.dma_start(out=vec_sb[:], in_=vec.rearrange("(p t) -> p t", t=PACK))
+        load_table(1)
+        nc.sync.dma_start(out=w2_raw[:], in_=w2_words.rearrange("a p c i -> p a (c i)").bitcast(I32))
+        load_wgs(0, CHUNK)
+        nc.sync.dma_start(idx2[:], offs2)
+        nc.sync.dma_start(out=page[0][:], in_=page_rows[0])
+        load_wgs(CHUNK, 2 * S)
+        nc.sync.dma_start(idx3[:], offs3)
+        nc.sync.dma_start(out=temp_sb[:], in_=temp.rearrange("(p t) -> p t", t=PACK))
+        nc.sync.dma_start(out=page[1][:], in_=page_rows[1])
+        load_wgs(2 * S, PACK * S)
+        for t in range(2, PACK):
+            nc.sync.dma_start(out=page[t][:], in_=page_rows[t])
+        nc.sync.dma_start(out=w3_raw[:], in_=w3.rearrange("(p j) n -> p j n", j=PACK))
+        nc.sync.dma_start(out=w4_codes[:].bitcast(I32), in_=w4_words[0].bitcast(I32))
+        load_scales(nc.sync, w4_sc, w4_scales)
+        with nc.allow_non_contiguous_dma(reason="one gain a partition"):
+            nc.sync.dma_start(out=gain2_sb[:], in_=gain2.rearrange("(u p) -> p u", p=P))
+        nc.sync.dma_start(out=mix_sb[:], in_=mix.rearrange("(p t) m -> p t m", t=PACK))
+        nc.sync.dma_start(out=prior_sb[:], in_=prior.rearrange("(u p) m -> p u m", p=P))
+
+        v_codes = [[held([P, CHUNK], U32, f"v_codes{a}_{c}") for c in range(CHUNKS)] for a in range(PASSES)]
+        v_sc = [held([P, CHUNK], U8, f"v_sc{c}") for c in range(CHUNKS)]
+
+        def gather_words(a, c):
+            nc.vector.tensor_copy(v_codes[a][c][:], tab[a][:].indirect(idx[:, list_cols(c)]))
+
+        def gather_scales(c):
+            nc.vector.tensor_copy(v_sc[c][:], tab_sc[:].indirect(idx[:, list_cols(c)]))
+
+        w1_bf = [held([P, PACK, P, PACK], BF16, f"w1_bf{a}") for a in range(PASSES)]
+        w1_codes = [held([P, H], U32, f"w1_codes{a}") for a in range(PASSES)]
+        w1_sc = [held([P, H], U8, f"w1_sc{a}") for a in range(PASSES)]
+
+        def w1_views(a, lo, hi):
+            return (
+                w1_bf[a][:].rearrange("p t m j -> p m j t")[:, lo:hi],
+                w1_raw[a][:].rearrange("p j (m t) -> p m j t", t=PACK)[:, lo:hi],
+            )
+
+        def quantize_w1(a):
+            nc.vector.quantize_mx(
+                out=w1_codes[a][:].bitcast(E4M3),
+                scales=w1_sc[a][:],
+                in_=w1_bf[a][:].rearrange("p t m j -> p (t m j)"),
+            )
+
+        w2_codes = held([P, PASSES, H], I32, "w2_codes")
+        w2_sc = held([P, H], U8, "w2_sc")
+
+        gather_words(0, 0)
+        gather_scales(0)
+        nc.scalar.copy(*w1_views(0, 0, P))
+        gather_words(0, 1)
+        gather_scales(1)
+        nc.vector.tensor_copy(
+            w2_sc[:].rearrange("p (t m) -> p t m", t=PACK),
+            w2_raw_sc[:].rearrange("p (m t) -> p t m", t=PACK),
+        )
+        nc.vector.tensor_copy(*w1_views(1, 0, P // 2))
+        nc.scalar.copy(*w1_views(1, P // 2, P))
+        quantize_w1(0)
+        quantize_w1(1)
+        gather_words(1, 0)
+        nc.scalar.copy(
+            w2_codes[:].bitcast(U32).rearrange("p a (t m) -> p a m t", t=PACK),
+            w2_raw[:].bitcast(U32).rearrange("p a (m t) -> p a m t", t=PACK),
+        )
+        gather_words(1, 1)
+
+        look = [held([P, PACK, CHUNK], F32, f"look{c}") for c in range(CHUNKS)]
+        top = held([P, PACK], F32, "top")
+        shift = held([P, PACK], F32, "shift")
+
+        for t in range(PACK):
+            rows = slice(t * P, (t + 1) * P)
+            row = slice(t, t + 1)
+            h = ring.tile([P, S], F32, tag="h")
+            for c in range(CHUNKS):
+                bent_ps = psum.tile([P, CHUNK], F32, tag="first")
+                line_ps = psum.tile([P, CHUNK], F32, tag="second")
+                for a in range(PASSES):
+                    nc.tensor.matmul_mx(
+                        out=bent_ps[:],
+                        lhsT=w1_codes[a][:, rows].bitcast(E4M3),
+                        lhsT_scale=w1_sc[a][:, rows],
+                        rhs=v_codes[a][c][:].bitcast(E4M3),
+                        rhs_scale=v_sc[c][4 * a :, :],
+                        start=(a == 0),
+                        stop=(a == PASSES - 1),
+                    )
+                for a in range(PASSES):
+                    nc.tensor.matmul_mx(
+                        out=line_ps[:],
+                        lhsT=w2_codes[:, a, rows].bitcast(E4M3),
+                        lhsT_scale=w2_sc[4 * a :, rows],
+                        rhs=v_codes[a][c][:].bitcast(E4M3),
+                        rhs_scale=v_sc[c][4 * a :, :],
+                        start=(a == 0),
+                        stop=(a == PASSES - 1),
+                    )
+                bent = ring.tile([P, CHUNK], F32, tag="bent")
+                nc.scalar.activation(out=bent[:], in_=bent_ps[:], func=ACT.Tanh)
+                biased = hring.tile([P, CHUNK], F32, tag="biased")
+                nc.scalar.activation(
+                    out=biased[:], in_=bent[:], func=ACT.Identity, scale=gain1_sb[:, row], bias=b2_sb[:, row]
+                )
+                nc.vector.tensor_tensor(h[:, chunk_cols(c)], line_ps[:], biased[:], ALU.add)
+                if t == 0:
+                    nc.vector.tensor_tensor(
+                        page[t][:].indirect(idx2[:, list_cols(c)]), h[:, chunk_cols(c)], wg[:, chunk_cols(c)], ALU.mult
+                    )
+            if t > 0:
+                nc.vector.tensor_tensor(page[t][:].indirect(idx2[:]), h[:], wg[:, t * S : (t + 1) * S], ALU.mult)
+            nc.vector.reduce_max(top[:, row], page[t][:], AXIS.X)
+            nc.vector.tensor_scalar(shift[:, row], top[:, row], temp_sb[:, row], -1.0, ALU.mult, ALU.mult)
+            for c in range(CHUNKS):
+                nc.scalar.activation(
+                    out=look[c][:, t, :],
+                    in_=page[t][:].indirect(idx3[:, list_cols(c)]),
+                    func=ACT.Exp,
+                    bias=shift[:, row],
+                    scale=temp_sb[:, row],
+                )
+
+        w3_bf = held([P, N, PACK], BF16, "w3_bf")
+        w3_codes = held([P, N], U32, "w3_codes")
+        w3_sc = held([P, N], U8, "w3_sc")
+        nc.scalar.copy(
+            w3_bf[:].rearrange("p (c i) j -> p c j i", i=4),
+            w3_raw[:].rearrange("p j (c i) -> p c j i", i=4),
+        )
+        nc.vector.quantize_mx(
+            out=w3_codes[:].bitcast(E4M3), scales=w3_sc[:], in_=w3_bf[:].rearrange("p n j -> p (n j)")
+        )
+        one = held([P, 1], F32, "one")
+        phase = held([P, 1], F32, "phase")
+        gain2_m2 = held([P, OUT_TILES], F32, "gain2_m2")
+        nc.gpsimd.memset(one[:], 1.0)
+        nc.gpsimd.tensor_scalar(phase[:], one[:], -math.pi / 4, 0.0, ALU.mult, ALU.add)
+        nc.gpsimd.tensor_scalar(gain2_m2[:], gain2_sb[:], -2.0, 0.0, ALU.mult, ALU.add)
+
+        x_codes, x_sc = [], []
+        for c in range(CHUNKS):
+            x_bf = ring.tile([P, CHUNK, PACK], BF16, tag="x_bf", align_bytes=64)
+            nc.vector.tensor_tensor(
+                x_bf[:].rearrange("p (g i) t -> p g t i", i=4),
+                look[c][:].rearrange("p t (g i) -> p g t i", i=4),
+                mix_sb[:, :, chunk_cols(c)].rearrange("p t (g i) -> p g t i", i=4),
+                ALU.mult,
+            )
+            x_codes.append(held([P, CHUNK], U32, f"x_codes{c}"))
+            x_sc.append(held([P, CHUNK], U8, f"x_sc{c}"))
+            nc.vector.quantize_mx(
+                out=x_codes[c][:].bitcast(E4M3), scales=x_sc[c][:], in_=x_bf[:].rearrange("p m t -> p (m t)")
+            )
+        for c in range(CHUNKS):
+            for u in range(OUT_TILES):
+                rows = slice(u * P, (u + 1) * P)
+                row = slice(u, u + 1)
+                wave_ps = psum.tile([P, CHUNK], F32, tag="first")
+                plain_ps = psum.tile([P, CHUNK], F32, tag="second")
+                nc.tensor.matmul_mx(
+                    out=wave_ps[:],
+                    lhsT=w3_codes[:, rows].bitcast(E4M3),
+                    lhsT_scale=w3_sc[:, rows],
+                    rhs=x_codes[c][:].bitcast(E4M3),
+                    rhs_scale=x_sc[c][:],
+                    start=True,
+                    stop=True,
+                )
+                nc.tensor.matmul_mx(
+                    out=plain_ps[:],
+                    lhsT=w4_codes[:, 2 * u * P : 2 * (u + 1) * P].bitcast(E2M1),
+                    lhsT_scale=w4_sc[:, rows],
+                    rhs=x_codes[c][:].bitcast(E4M3),
+                    rhs_scale=x_sc[c][:],
+                    start=True,
+                    stop=True,
+                )
+                score = tail.tile([P, CHUNK], F32, tag="score")
+                nc.scalar.activation(out=score[:], in_=wave_ps[:], func=ACT.Sin, scale=0.5, bias=phase[:])
+                nc.scalar.activation(out=score[:], in_=score[:], func=ACT.Square)
+                nc.vector.scalar_tensor_tensor(
+                    score[:], score[:], gain2_m2[:, row], plain_ps[:], ALU.mult, ALU.add
+                )
+                nc.vector.scalar_tensor_tensor(
+                    score[:], score[:], gain2_sb[:, row], prior_sb[:, u, chunk_cols(c)], ALU.add, ALU.add
+                )
+                nc.sync.dma_start(out=out[rows, chunk_cols(c)], in_=score[:])

@@ -36,7 +36,6 @@ def tile_list_flux_reread_scores_kernel(
     with ExitStack() as ctx:
         keep = ctx.enter_context(tc.tile_pool(name="keep", bufs=1))
         ring = ctx.enter_context(tc.tile_pool(name="ring", bufs=2))
-        hring = ctx.enter_context(tc.tile_pool(name="hring", bufs=4))
         tail = ctx.enter_context(tc.tile_pool(name="tail", bufs=CHUNKS * OUT_TILES))
         psum = ctx.enter_context(tc.psum_pool(name="psum", bufs=4))
 
@@ -98,7 +97,7 @@ def tile_list_flux_reread_scores_kernel(
 
         nc.sync.dma_start(idx[:], offs)
         load_table(0)
-        load_scales(nc.scalar, tab_sc, tab_scales)
+        load_scales(nc.sync, tab_sc, tab_scales)
         load_w1(0)
         load_w1(1)
         load_scales(nc.sync, w2_raw_sc, w2_scales)
@@ -113,10 +112,10 @@ def tile_list_flux_reread_scores_kernel(
         nc.sync.dma_start(idx3[:], offs3)
         nc.sync.dma_start(out=temp_sb[:], in_=temp.rearrange("(p t) -> p t", t=PACK))
         nc.sync.dma_start(out=page[1][:], in_=page_rows[1])
+        nc.sync.dma_start(out=w3_raw[:], in_=w3.rearrange("(p j) n -> p j n", j=PACK))
         load_wgs(2 * S, PACK * S)
         for t in range(2, PACK):
             nc.sync.dma_start(out=page[t][:], in_=page_rows[t])
-        nc.sync.dma_start(out=w3_raw[:], in_=w3.rearrange("(p j) n -> p j n", j=PACK))
         nc.sync.dma_start(out=w4_codes[:].bitcast(I32), in_=w4_words[0].bitcast(I32))
         load_scales(nc.sync, w4_sc, w4_scales)
         with nc.allow_non_contiguous_dma(reason="one gain a partition"):
@@ -180,7 +179,9 @@ def tile_list_flux_reread_scores_kernel(
         for t in range(PACK):
             rows = slice(t * P, (t + 1) * P)
             row = slice(t, t + 1)
-            h = ring.tile([P, S], F32, tag="h")
+            h = keep.tile([P, S], F32, tag="h")
+            biased = ring.tile([P, S], F32, tag="biased")
+            line = ring.tile([P, S], F32, tag="line", name="line") if t > 0 else None
             for c in range(CHUNKS):
                 bent_ps = psum.tile([P, CHUNK], F32, tag="first")
                 line_ps = psum.tile([P, CHUNK], F32, tag="second")
@@ -204,18 +205,19 @@ def tile_list_flux_reread_scores_kernel(
                         start=(a == 0),
                         stop=(a == PASSES - 1),
                     )
-                bent = ring.tile([P, CHUNK], F32, tag="bent")
-                nc.scalar.activation(out=bent[:], in_=bent_ps[:], func=ACT.Tanh)
-                biased = hring.tile([P, CHUNK], F32, tag="biased")
+                cols = chunk_cols(c)
+                nc.scalar.activation(out=biased[:, cols], in_=bent_ps[:], func=ACT.Tanh)
                 nc.scalar.activation(
-                    out=biased[:], in_=bent[:], func=ACT.Identity, scale=gain1_sb[:, row], bias=b2_sb[:, row]
+                    out=biased[:, cols], in_=biased[:, cols], func=ACT.Identity,
+                    scale=gain1_sb[:, row], bias=b2_sb[:, row],
                 )
-                nc.vector.tensor_tensor(h[:, chunk_cols(c)], line_ps[:], biased[:], ALU.add)
                 if t == 0:
-                    nc.vector.tensor_tensor(
-                        page[t][:].indirect(idx2[:, list_cols(c)]), h[:, chunk_cols(c)], wg[:, chunk_cols(c)], ALU.mult
-                    )
+                    nc.vector.tensor_tensor(h[:, cols], line_ps[:], biased[:, cols], ALU.add)
+                    nc.vector.tensor_tensor(page[t][:].indirect(idx2[:, list_cols(c)]), h[:, cols], wg[:, cols], ALU.mult)
+                else:
+                    nc.scalar.copy(line[:, cols], line_ps[:])
             if t > 0:
+                nc.gpsimd.tensor_tensor(h[:], line[:], biased[:], ALU.add)
                 nc.vector.tensor_tensor(page[t][:].indirect(idx2[:]), h[:], wg[:, t * S : (t + 1) * S], ALU.mult)
             nc.vector.reduce_max(top[:, row], page[t][:], AXIS.X)
             nc.vector.tensor_scalar(shift[:, row], top[:, row], temp_sb[:, row], -1.0, ALU.mult, ALU.mult)

@@ -35,7 +35,6 @@ def tile_list_flux_reread_scores_kernel(
     nc = tc.nc
     with ExitStack() as ctx:
         keep = ctx.enter_context(tc.tile_pool(name="keep", bufs=1))
-        ring = ctx.enter_context(tc.tile_pool(name="ring", bufs=2))
         tail = ctx.enter_context(tc.tile_pool(name="tail", bufs=CHUNKS * OUT_TILES))
         psum = ctx.enter_context(tc.psum_pool(name="psum", bufs=4))
 
@@ -71,10 +70,10 @@ def tile_list_flux_reread_scores_kernel(
         for plane in (tab_sc, w2_raw_sc, w4_sc):
             nc.gpsimd.memset(plane[:].bitcast(I32), 0)
 
-        def load_scales(queue, plane, scales):
+        def load_scales(plane, scales):
             rows = 4 * scales.shape[0]
             for q in range(QUADS):
-                queue.dma_start(
+                nc.sync.dma_start(
                     out=plane[32 * q : 32 * q + rows, :].bitcast(I32),
                     in_=scales[:, 4 * q : 4 * q + 4, :].bitcast(I32),
                 )
@@ -92,15 +91,15 @@ def tile_list_flux_reread_scores_kernel(
         wgs_rows = wgs.rearrange("(q t) j -> q (t j)", t=PACK)
 
         def load_wgs(lo, hi):
-            for q in range(QUADS):
+            for q in (0, 2, 1, 3):
                 nc.sync.dma_start(out=wg[32 * q : 32 * q + 32, lo:hi], in_=wgs_rows[:, lo:hi])
 
         nc.sync.dma_start(idx[:], offs)
         load_table(0)
-        load_scales(nc.sync, tab_sc, tab_scales)
+        load_scales(tab_sc, tab_scales)
         load_w1(0)
         load_w1(1)
-        load_scales(nc.sync, w2_raw_sc, w2_scales)
+        load_scales(w2_raw_sc, w2_scales)
         for vec_sb, vec in ((gain1_sb, gain1), (b2_sb, b2)):
             nc.sync.dma_start(out=vec_sb[:], in_=vec.rearrange("(p t) -> p t", t=PACK))
         load_table(1)
@@ -108,16 +107,17 @@ def tile_list_flux_reread_scores_kernel(
         load_wgs(0, CHUNK)
         nc.sync.dma_start(idx2[:], offs2)
         nc.sync.dma_start(out=page[0][:], in_=page_rows[0])
-        load_wgs(CHUNK, 2 * S)
-        nc.sync.dma_start(idx3[:], offs3)
+        load_wgs(CHUNK, S)
         nc.sync.dma_start(out=temp_sb[:], in_=temp.rearrange("(p t) -> p t", t=PACK))
         nc.sync.dma_start(out=page[1][:], in_=page_rows[1])
+        load_wgs(S, 2 * S)
         nc.sync.dma_start(out=w3_raw[:], in_=w3.rearrange("(p j) n -> p j n", j=PACK))
         load_wgs(2 * S, PACK * S)
         for t in range(2, PACK):
             nc.sync.dma_start(out=page[t][:], in_=page_rows[t])
+        nc.sync.dma_start(idx3[:], offs3)
         nc.sync.dma_start(out=w4_codes[:].bitcast(I32), in_=w4_words[0].bitcast(I32))
-        load_scales(nc.sync, w4_sc, w4_scales)
+        load_scales(w4_sc, w4_scales)
         with nc.allow_non_contiguous_dma(reason="one gain a partition"):
             nc.sync.dma_start(out=gain2_sb[:], in_=gain2.rearrange("(u p) -> p u", p=P))
         nc.sync.dma_start(out=mix_sb[:], in_=mix.rearrange("(p t) m -> p t m", t=PACK))
@@ -175,15 +175,15 @@ def tile_list_flux_reread_scores_kernel(
         look = [held([P, PACK, CHUNK], F32, f"look{c}") for c in range(CHUNKS)]
         top = held([P, PACK], F32, "top")
         shift = held([P, PACK], F32, "shift")
+        temp_neg = held([P, PACK], F32, "temp_neg")
+        nc.scalar.activation(out=temp_neg[:], in_=temp_sb[:], func=ACT.Copy, scale=-1.0)
 
         for t in range(PACK):
             rows = slice(t * P, (t + 1) * P)
             row = slice(t, t + 1)
-            h = keep.tile([P, S], F32, tag="h")
-            biased = ring.tile([P, S], F32, tag="biased")
-            line = ring.tile([P, S], F32, tag="line", name="line") if t > 0 else None
+            h = held([P, S], F32, f"h{t}")
             for c in range(CHUNKS):
-                bent_ps = psum.tile([P, CHUNK], F32, tag="first")
+                bent_ps = psum.tile([P, CHUNK], F32, tag="first", bufs=2)
                 line_ps = psum.tile([P, CHUNK], F32, tag="second")
                 for a in range(PASSES):
                     nc.tensor.matmul_mx(
@@ -206,21 +206,25 @@ def tile_list_flux_reread_scores_kernel(
                         stop=(a == PASSES - 1),
                     )
                 cols = chunk_cols(c)
-                nc.scalar.activation(out=biased[:, cols], in_=bent_ps[:], func=ACT.Tanh)
-                nc.scalar.activation(
-                    out=biased[:, cols], in_=biased[:, cols], func=ACT.Identity,
-                    scale=gain1_sb[:, row], bias=b2_sb[:, row],
-                )
+                nc.scalar.activation(out=h[:, cols], in_=bent_ps[:], func=ACT.Tanh)
                 if t == 0:
-                    nc.vector.tensor_tensor(h[:, cols], line_ps[:], biased[:, cols], ALU.add)
-                    nc.vector.tensor_tensor(page[t][:].indirect(idx2[:, list_cols(c)]), h[:, cols], wg[:, cols], ALU.mult)
+                    nc.vector.tensor_scalar(
+                        h[:, cols], h[:, cols], gain1_sb[:, row], b2_sb[:, row], ALU.mult, ALU.add
+                    )
                 else:
-                    nc.scalar.copy(line[:, cols], line_ps[:])
+                    nc.scalar.activation(
+                        out=h[:, cols], in_=h[:, cols], func=ACT.Identity,
+                        scale=gain1_sb[:, row], bias=b2_sb[:, row],
+                    )
+                nc.vector.tensor_tensor(h[:, cols], line_ps[:], h[:, cols], ALU.add)
+                if t == 0:
+                    nc.vector.tensor_tensor(
+                        page[t][:].indirect(idx2[:, list_cols(c)]), h[:, cols], wg[:, cols], ALU.mult
+                    )
             if t > 0:
-                nc.gpsimd.tensor_tensor(h[:], line[:], biased[:], ALU.add)
                 nc.vector.tensor_tensor(page[t][:].indirect(idx2[:]), h[:], wg[:, t * S : (t + 1) * S], ALU.mult)
             nc.vector.reduce_max(top[:, row], page[t][:], AXIS.X)
-            nc.vector.tensor_scalar(shift[:, row], top[:, row], temp_sb[:, row], -1.0, ALU.mult, ALU.mult)
+            nc.scalar.activation(out=shift[:, row], in_=top[:, row], func=ACT.Copy, scale=temp_neg[:, row])
             for c in range(CHUNKS):
                 nc.scalar.activation(
                     out=look[c][:, t, :],
@@ -245,11 +249,11 @@ def tile_list_flux_reread_scores_kernel(
         gain2_m2 = held([P, OUT_TILES], F32, "gain2_m2")
         nc.gpsimd.memset(one[:], 1.0)
         nc.gpsimd.tensor_scalar(phase[:], one[:], -math.pi / 4, 0.0, ALU.mult, ALU.add)
-        nc.gpsimd.tensor_scalar(gain2_m2[:], gain2_sb[:], -2.0, 0.0, ALU.mult, ALU.add)
+        nc.scalar.activation(out=gain2_m2[:], in_=gain2_sb[:], func=ACT.Copy, scale=-2.0)
 
         x_codes, x_sc = [], []
         for c in range(CHUNKS):
-            x_bf = ring.tile([P, CHUNK, PACK], BF16, tag="x_bf", align_bytes=64)
+            x_bf = keep.tile([P, CHUNK, PACK], BF16, tag="x_bf", align_bytes=64)
             nc.vector.tensor_tensor(
                 x_bf[:].rearrange("p (g i) t -> p g t i", i=4),
                 look[c][:].rearrange("p t (g i) -> p g t i", i=4),
@@ -265,7 +269,7 @@ def tile_list_flux_reread_scores_kernel(
             for u in range(OUT_TILES):
                 rows = slice(u * P, (u + 1) * P)
                 row = slice(u, u + 1)
-                wave_ps = psum.tile([P, CHUNK], F32, tag="first")
+                wave_ps = psum.tile([P, CHUNK], F32, tag="first", bufs=2)
                 plain_ps = psum.tile([P, CHUNK], F32, tag="second")
                 nc.tensor.matmul_mx(
                     out=wave_ps[:],

@@ -23,9 +23,14 @@ PACK = 4
 PASSES = K // (P * PACK)
 CHUNK = 512
 CHUNKS = S // CHUNK
-LIST_COLS = CHUNK // 16
-QUADS = 4
+GROUP = 16
+QUAD = 32
+QUADS = P // QUAD
+BLOCKS = 4
+LINE = 4
 OUT_TILES = N // P
+FUNCTION_BANKS = 2
+PLAIN_BANKS = 4
 
 
 def tile_list_flux_reread_scores_kernel(
@@ -35,8 +40,9 @@ def tile_list_flux_reread_scores_kernel(
     nc = tc.nc
     with ExitStack() as ctx:
         keep = ctx.enter_context(tc.tile_pool(name="keep", bufs=1))
+        ring = ctx.enter_context(tc.tile_pool(name="ring", bufs=2))
         tail = ctx.enter_context(tc.tile_pool(name="tail", bufs=CHUNKS * OUT_TILES))
-        psum = ctx.enter_context(tc.psum_pool(name="psum", bufs=4))
+        psum = ctx.enter_context(tc.psum_pool(name="psum", bufs=PLAIN_BANKS))
 
         def held(shape, dtype, name):
             return keep.tile(shape, dtype, name=name, align_bytes=64)
@@ -45,11 +51,11 @@ def tile_list_flux_reread_scores_kernel(
             return slice(c * CHUNK, (c + 1) * CHUNK)
 
         def list_cols(c):
-            return slice(c * LIST_COLS, (c + 1) * LIST_COLS)
+            return slice(c * CHUNK // GROUP, (c + 1) * CHUNK // GROUP)
 
-        idx = held([P, S // 16], U16, "idx")
-        idx2 = held([P, S // 16], U16, "idx2")
-        idx3 = held([P, M // 16], U16, "idx3")
+        idx = held([P, S // GROUP], U16, "idx")
+        idx2 = held([P, S // GROUP], U16, "idx2")
+        idx3 = held([P, M // GROUP], U16, "idx3")
         tab = [held([P, T], U32, f"tab{a}") for a in range(PASSES)]
         tab_sc = held([P, T], U8, "tab_sc")
         w1_raw = [held([P, PACK, H], F32, f"w1_raw{a}") for a in range(PASSES)]
@@ -67,15 +73,15 @@ def tile_list_flux_reread_scores_kernel(
         temp_sb = held([P, PACK], F32, "temp_sb")
         gain2_sb = held([P, OUT_TILES], F32, "gain2_sb")
 
-        for plane in (tab_sc, w2_raw_sc, w4_sc):
-            nc.gpsimd.memset(plane[:].bitcast(I32), 0)
+        for scale_tile in (tab_sc, w2_raw_sc, w4_sc):
+            nc.gpsimd.memset(scale_tile[:].bitcast(I32), 0)
 
-        def load_scales(plane, scales):
-            rows = 4 * scales.shape[0]
+        def load_scales(scale_tile, scales):
+            live = BLOCKS * scales.shape[0]
             for q in range(QUADS):
                 nc.sync.dma_start(
-                    out=plane[32 * q : 32 * q + rows, :].bitcast(I32),
-                    in_=scales[:, 4 * q : 4 * q + 4, :].bitcast(I32),
+                    out=scale_tile[QUAD * q : QUAD * q + live, :].bitcast(I32),
+                    in_=scales[:, BLOCKS * q : BLOCKS * (q + 1), :].bitcast(I32),
                 )
 
         def load_table(a):
@@ -84,15 +90,15 @@ def tile_list_flux_reread_scores_kernel(
             )
 
         def load_w1(a):
-            rows = w1[a * P * PACK : (a + 1) * P * PACK, :]
-            nc.sync.dma_start(out=w1_raw[a][:], in_=rows.rearrange("(p j) c -> p j c", j=PACK))
+            k_rows = w1[a * P * PACK : (a + 1) * P * PACK, :]
+            nc.sync.dma_start(out=w1_raw[a][:], in_=k_rows.rearrange("(p j) c -> p j c", j=PACK))
 
         page_rows = page0.rearrange("(p t) c -> t p c", t=PACK)
         wgs_rows = wgs.rearrange("(q t) j -> q (t j)", t=PACK)
 
         def load_wgs(lo, hi):
             for q in (0, 2, 1, 3):
-                nc.sync.dma_start(out=wg[32 * q : 32 * q + 32, lo:hi], in_=wgs_rows[:, lo:hi])
+                nc.sync.dma_start(out=wg[QUAD * q : QUAD * (q + 1), lo:hi], in_=wgs_rows[:, lo:hi])
 
         nc.sync.dma_start(idx[:], offs)
         load_table(0)
@@ -112,13 +118,13 @@ def tile_list_flux_reread_scores_kernel(
         nc.sync.dma_start(out=page[1][:], in_=page_rows[1])
         load_wgs(S, 2 * S)
         nc.sync.dma_start(out=w3_raw[:], in_=w3.rearrange("(p j) n -> p j n", j=PACK))
+        nc.sync.dma_start(idx3[:], offs3)
         load_wgs(2 * S, PACK * S)
         for t in range(2, PACK):
             nc.sync.dma_start(out=page[t][:], in_=page_rows[t])
-        nc.sync.dma_start(idx3[:], offs3)
         nc.sync.dma_start(out=w4_codes[:].bitcast(I32), in_=w4_words[0].bitcast(I32))
         load_scales(w4_sc, w4_scales)
-        with nc.allow_non_contiguous_dma(reason="one gain a partition"):
+        with nc.allow_non_contiguous_dma(reason="one gain for each partition and output tile"):
             nc.sync.dma_start(out=gain2_sb[:], in_=gain2.rearrange("(u p) -> p u", p=P))
         nc.sync.dma_start(out=mix_sb[:], in_=mix.rearrange("(p t) m -> p t m", t=PACK))
         nc.sync.dma_start(out=prior_sb[:], in_=prior.rearrange("(u p) m -> p u m", p=P))
@@ -179,67 +185,73 @@ def tile_list_flux_reread_scores_kernel(
         nc.scalar.activation(out=temp_neg[:], in_=temp_sb[:], func=ACT.Copy, scale=-1.0)
 
         for t in range(PACK):
-            rows = slice(t * P, (t + 1) * P)
-            row = slice(t, t + 1)
-            h = held([P, S], F32, f"h{t}")
+            first_tile = t == 0
+            r_cols = slice(t * P, (t + 1) * P)
+            vec_col = slice(t, t + 1)
+            h = keep.tile([P, S], F32, tag="h")
+            bent = ring.tile([P, S], F32, tag="bent")
+            linear = None if first_tile else ring.tile([P, S], F32, tag="linear", name="linear")
             for c in range(CHUNKS):
-                bent_ps = psum.tile([P, CHUNK], F32, tag="first", bufs=2)
-                line_ps = psum.tile([P, CHUNK], F32, tag="second")
+                bent_ps = psum.tile([P, CHUNK], F32, tag="function", bufs=FUNCTION_BANKS)
+                linear_ps = psum.tile([P, CHUNK], F32, tag="plain")
                 for a in range(PASSES):
                     nc.tensor.matmul_mx(
                         out=bent_ps[:],
-                        lhsT=w1_codes[a][:, rows].bitcast(E4M3),
-                        lhsT_scale=w1_sc[a][:, rows],
+                        lhsT=w1_codes[a][:, r_cols].bitcast(E4M3),
+                        lhsT_scale=w1_sc[a][:, r_cols],
                         rhs=v_codes[a][c][:].bitcast(E4M3),
-                        rhs_scale=v_sc[c][4 * a :, :],
+                        rhs_scale=v_sc[c][BLOCKS * a :, :],
                         start=(a == 0),
                         stop=(a == PASSES - 1),
                     )
                 for a in range(PASSES):
                     nc.tensor.matmul_mx(
-                        out=line_ps[:],
-                        lhsT=w2_codes[:, a, rows].bitcast(E4M3),
-                        lhsT_scale=w2_sc[4 * a :, rows],
+                        out=linear_ps[:],
+                        lhsT=w2_codes[:, a, r_cols].bitcast(E4M3),
+                        lhsT_scale=w2_sc[BLOCKS * a :, r_cols],
                         rhs=v_codes[a][c][:].bitcast(E4M3),
-                        rhs_scale=v_sc[c][4 * a :, :],
+                        rhs_scale=v_sc[c][BLOCKS * a :, :],
                         start=(a == 0),
                         stop=(a == PASSES - 1),
                     )
                 cols = chunk_cols(c)
-                nc.scalar.activation(out=h[:, cols], in_=bent_ps[:], func=ACT.Tanh)
-                if t == 0:
+                nc.scalar.activation(out=bent[:, cols], in_=bent_ps[:], func=ACT.Tanh)
+                if first_tile:
                     nc.vector.tensor_scalar(
-                        h[:, cols], h[:, cols], gain1_sb[:, row], b2_sb[:, row], ALU.mult, ALU.add
+                        bent[:, cols], bent[:, cols], gain1_sb[:, vec_col], b2_sb[:, vec_col], ALU.mult, ALU.add
                     )
-                else:
-                    nc.scalar.activation(
-                        out=h[:, cols], in_=h[:, cols], func=ACT.Identity,
-                        scale=gain1_sb[:, row], bias=b2_sb[:, row],
-                    )
-                nc.vector.tensor_tensor(h[:, cols], line_ps[:], h[:, cols], ALU.add)
-                if t == 0:
+                    nc.vector.tensor_tensor(h[:, cols], linear_ps[:], bent[:, cols], ALU.add)
                     nc.vector.tensor_tensor(
                         page[t][:].indirect(idx2[:, list_cols(c)]), h[:, cols], wg[:, cols], ALU.mult
                     )
-            if t > 0:
+                else:
+                    nc.scalar.activation(
+                        out=bent[:, cols], in_=bent[:, cols], func=ACT.Identity,
+                        scale=gain1_sb[:, vec_col], bias=b2_sb[:, vec_col],
+                    )
+                    nc.scalar.copy(linear[:, cols], linear_ps[:])
+            if not first_tile:
+                nc.gpsimd.tensor_tensor(h[:], linear[:], bent[:], ALU.add)
                 nc.vector.tensor_tensor(page[t][:].indirect(idx2[:]), h[:], wg[:, t * S : (t + 1) * S], ALU.mult)
-            nc.vector.reduce_max(top[:, row], page[t][:], AXIS.X)
-            nc.scalar.activation(out=shift[:, row], in_=top[:, row], func=ACT.Copy, scale=temp_neg[:, row])
+            nc.vector.reduce_max(top[:, vec_col], page[t][:], AXIS.X)
+            nc.scalar.activation(
+                out=shift[:, vec_col], in_=top[:, vec_col], func=ACT.Copy, scale=temp_neg[:, vec_col]
+            )
             for c in range(CHUNKS):
                 nc.scalar.activation(
                     out=look[c][:, t, :],
                     in_=page[t][:].indirect(idx3[:, list_cols(c)]),
                     func=ACT.Exp,
-                    bias=shift[:, row],
-                    scale=temp_sb[:, row],
+                    bias=shift[:, vec_col],
+                    scale=temp_sb[:, vec_col],
                 )
 
         w3_bf = held([P, N, PACK], BF16, "w3_bf")
         w3_codes = held([P, N], U32, "w3_codes")
         w3_sc = held([P, N], U8, "w3_sc")
         nc.scalar.copy(
-            w3_bf[:].rearrange("p (c i) j -> p c j i", i=4),
-            w3_raw[:].rearrange("p j (c i) -> p c j i", i=4),
+            w3_bf[:].rearrange("p (g i) j -> p g j i", i=LINE),
+            w3_raw[:].rearrange("p j (g i) -> p g j i", i=LINE),
         )
         nc.vector.quantize_mx(
             out=w3_codes[:].bitcast(E4M3), scales=w3_sc[:], in_=w3_bf[:].rearrange("p n j -> p (n j)")
@@ -255,9 +267,9 @@ def tile_list_flux_reread_scores_kernel(
         for c in range(CHUNKS):
             x_bf = keep.tile([P, CHUNK, PACK], BF16, tag="x_bf", align_bytes=64)
             nc.vector.tensor_tensor(
-                x_bf[:].rearrange("p (g i) t -> p g t i", i=4),
-                look[c][:].rearrange("p t (g i) -> p g t i", i=4),
-                mix_sb[:, :, chunk_cols(c)].rearrange("p t (g i) -> p g t i", i=4),
+                x_bf[:].rearrange("p (g i) t -> p g t i", i=LINE),
+                look[c][:].rearrange("p t (g i) -> p g t i", i=LINE),
+                mix_sb[:, :, chunk_cols(c)].rearrange("p t (g i) -> p g t i", i=LINE),
                 ALU.mult,
             )
             x_codes.append(held([P, CHUNK], U32, f"x_codes{c}"))
@@ -265,16 +277,17 @@ def tile_list_flux_reread_scores_kernel(
             nc.vector.quantize_mx(
                 out=x_codes[c][:].bitcast(E4M3), scales=x_sc[c][:], in_=x_bf[:].rearrange("p m t -> p (m t)")
             )
+
         for c in range(CHUNKS):
             for u in range(OUT_TILES):
-                rows = slice(u * P, (u + 1) * P)
-                row = slice(u, u + 1)
-                wave_ps = psum.tile([P, CHUNK], F32, tag="first", bufs=2)
-                plain_ps = psum.tile([P, CHUNK], F32, tag="second")
+                n_cols = slice(u * P, (u + 1) * P)
+                gain_col = slice(u, u + 1)
+                wave_ps = psum.tile([P, CHUNK], F32, tag="function", bufs=FUNCTION_BANKS)
+                plain_ps = psum.tile([P, CHUNK], F32, tag="plain")
                 nc.tensor.matmul_mx(
                     out=wave_ps[:],
-                    lhsT=w3_codes[:, rows].bitcast(E4M3),
-                    lhsT_scale=w3_sc[:, rows],
+                    lhsT=w3_codes[:, n_cols].bitcast(E4M3),
+                    lhsT_scale=w3_sc[:, n_cols],
                     rhs=x_codes[c][:].bitcast(E4M3),
                     rhs_scale=x_sc[c][:],
                     start=True,
@@ -283,7 +296,7 @@ def tile_list_flux_reread_scores_kernel(
                 nc.tensor.matmul_mx(
                     out=plain_ps[:],
                     lhsT=w4_codes[:, 2 * u * P : 2 * (u + 1) * P].bitcast(E2M1),
-                    lhsT_scale=w4_sc[:, rows],
+                    lhsT_scale=w4_sc[:, n_cols],
                     rhs=x_codes[c][:].bitcast(E4M3),
                     rhs_scale=x_sc[c][:],
                     start=True,
@@ -293,9 +306,9 @@ def tile_list_flux_reread_scores_kernel(
                 nc.scalar.activation(out=score[:], in_=wave_ps[:], func=ACT.Sin, scale=0.5, bias=phase[:])
                 nc.scalar.activation(out=score[:], in_=score[:], func=ACT.Square)
                 nc.vector.scalar_tensor_tensor(
-                    score[:], score[:], gain2_m2[:, row], plain_ps[:], ALU.mult, ALU.add
+                    score[:], score[:], gain2_m2[:, gain_col], plain_ps[:], ALU.mult, ALU.add
                 )
                 nc.vector.scalar_tensor_tensor(
-                    score[:], score[:], gain2_sb[:, row], prior_sb[:, u, chunk_cols(c)], ALU.add, ALU.add
+                    score[:], score[:], gain2_sb[:, gain_col], prior_sb[:, u, chunk_cols(c)], ALU.add, ALU.add
                 )
-                nc.sync.dma_start(out=out[rows, chunk_cols(c)], in_=score[:])
+                nc.sync.dma_start(out=out[n_cols, chunk_cols(c)], in_=score[:])

import math
from contextlib import ExitStack

import concourse.mybir as mybir

K, T, S, T2, M, H, N = 1024, 2048, 1024, 2048, 1024, 512, 384
FLOPS = 2 * (2 * K * H * S + 2 * H * N * M)

F32 = mybir.dt.float32
BF16 = mybir.dt.bfloat16
I32 = mybir.dt.int32
U32 = mybir.dt.uint32
U16 = mybir.dt.uint16
U8 = mybir.dt.uint8
E4M3 = mybir.dt.float8_e4m3fn_x4
E2M1 = mybir.dt.float4_e2m1fn_x4
ACT = mybir.ActivationFunctionType
ALU = mybir.AluOpType
AXIS = mybir.AxisListType

P = 128
PACK = 4
PASSES = K // (P * PACK)
CHUNK = 512
CHUNKS = S // CHUNK
GROUP = 16
QUAD = 32
QUADS = P // QUAD
BLOCKS = 4
LINE = 4
OUT_TILES = N // P
FUNCTION_BANKS = 2
PLAIN_BANKS = 4


def tile_list_flux_reread_scores_kernel(
    tc, tab_words, tab_scales, offs, offs2, offs3, w1, gain1, w2_words, w2_scales, b2,
    page0, wgs, temp, mix, w3, gain2, w4_words, w4_scales, prior, out,
):
    nc = tc.nc
    with ExitStack() as ctx:
        keep = ctx.enter_context(tc.tile_pool(name="keep", bufs=1))
        ring = ctx.enter_context(tc.tile_pool(name="ring", bufs=2))
        tail = ctx.enter_context(tc.tile_pool(name="tail", bufs=CHUNKS * OUT_TILES))
        psum = ctx.enter_context(tc.psum_pool(name="psum", bufs=PLAIN_BANKS))

        def held(shape, dtype, name):
            return keep.tile(shape, dtype, name=name, align_bytes=64)

        def chunk_cols(c):
            return slice(c * CHUNK, (c + 1) * CHUNK)

        def list_cols(c):
            return slice(c * CHUNK // GROUP, (c + 1) * CHUNK // GROUP)

        idx = held([P, S // GROUP], U16, "idx")
        idx2 = held([P, S // GROUP], U16, "idx2")
        idx3 = held([P, M // GROUP], U16, "idx3")
        tab = [held([P, T], U32, f"tab{a}") for a in range(PASSES)]
        tab_sc = held([P, T], U8, "tab_sc")
        w1_raw = [held([P, PACK, H], F32, f"w1_raw{a}") for a in range(PASSES)]
        w2_raw = held([P, PASSES, H], I32, "w2_raw")
        w2_raw_sc = held([P, H], U8, "w2_raw_sc")
        w4_codes = held([P, 2 * N], U8, "w4_codes")
        w4_sc = held([P, N], U8, "w4_sc")
        page = [held([P, T2], F32, f"page{t}") for t in range(PACK)]
        wg = held([P, PACK * S], F32, "wg")
        mix_sb = held([P, PACK, M], F32, "mix_sb")
        w3_raw = held([P, PACK, N], F32, "w3_raw")
        prior_sb = held([P, OUT_TILES, M], F32, "prior_sb")
        gain1_sb = held([P, PACK], F32, "gain1_sb")
        b2_sb = held([P, PACK], F32, "b2_sb")
        temp_sb = held([P, PACK], F32, "temp_sb")
        gain2_sb = held([P, OUT_TILES], F32, "gain2_sb")

        for scale_tile in (tab_sc, w2_raw_sc, w4_sc):
            nc.gpsimd.memset(scale_tile[:].bitcast(I32), 0)

        def load_scales(scale_tile, scales):
            live = BLOCKS * scales.shape[0]
            for q in range(QUADS):
                nc.sync.dma_start(
                    out=scale_tile[QUAD * q : QUAD * q + live, :].bitcast(I32),
                    in_=scales[:, BLOCKS * q : BLOCKS * (q + 1), :].bitcast(I32),
                )

        def load_table(a):
            nc.sync.dma_start(
                out=tab[a][:].bitcast(I32), in_=tab_words[a].rearrange("p t i -> p (t i)").bitcast(I32)
            )

        def load_w1(a):
            k_rows = w1[a * P * PACK : (a + 1) * P * PACK, :]
            nc.sync.dma_start(out=w1_raw[a][:], in_=k_rows.rearrange("(p j) c -> p j c", j=PACK))

        page_rows = page0.rearrange("(p t) c -> t p c", t=PACK)
        wgs_rows = wgs.rearrange("(q t) j -> q (t j)", t=PACK)

        def load_wgs(lo, hi):
            for q in (0, 2, 1, 3):
                nc.sync.dma_start(out=wg[QUAD * q : QUAD * (q + 1), lo:hi], in_=wgs_rows[:, lo:hi])

        nc.sync.dma_start(idx[:], offs)
        load_table(0)
        load_scales(tab_sc, tab_scales)
        load_w1(0)
        load_w1(1)
        load_scales(w2_raw_sc, w2_scales)
        for vec_sb, vec in ((gain1_sb, gain1), (b2_sb, b2)):
            nc.sync.dma_start(out=vec_sb[:], in_=vec.rearrange("(p t) -> p t", t=PACK))
        load_table(1)
        nc.sync.dma_start(out=w2_raw[:], in_=w2_words.rearrange("a p c i -> p a (c i)").bitcast(I32))
        load_wgs(0, CHUNK)
        nc.sync.dma_start(idx2[:], offs2)
        nc.sync.dma_start(out=page[0][:], in_=page_rows[0])
        load_wgs(CHUNK, S)
        nc.sync.dma_start(out=temp_sb[:], in_=temp.rearrange("(p t) -> p t", t=PACK))
        nc.sync.dma_start(out=page[1][:], in_=page_rows[1])
        load_wgs(S, 2 * S)
        nc.sync.dma_start(out=w3_raw[:], in_=w3.rearrange("(p j) n -> p j n", j=PACK))
        nc.sync.dma_start(idx3[:], offs3)
        load_wgs(2 * S, PACK * S)
        for t in range(2, PACK):
            nc.sync.dma_start(out=page[t][:], in_=page_rows[t])
        nc.sync.dma_start(out=w4_codes[:].bitcast(I32), in_=w4_words[0].bitcast(I32))
        load_scales(w4_sc, w4_scales)
        with nc.allow_non_contiguous_dma(reason="one gain for each partition and output tile"):
            nc.sync.dma_start(out=gain2_sb[:], in_=gain2.rearrange("(u p) -> p u", p=P))
        nc.sync.dma_start(out=mix_sb[:], in_=mix.rearrange("(p t) m -> p t m", t=PACK))
        nc.sync.dma_start(out=prior_sb[:], in_=prior.rearrange("(u p) m -> p u m", p=P))

        v_codes = [[held([P, CHUNK], U32, f"v_codes{a}_{c}") for c in range(CHUNKS)] for a in range(PASSES)]
        v_sc = [held([P, CHUNK], U8, f"v_sc{c}") for c in range(CHUNKS)]

        def gather_words(a, c):
            nc.vector.tensor_copy(v_codes[a][c][:], tab[a][:].indirect(idx[:, list_cols(c)]))

        def gather_scales(c):
            nc.vector.tensor_copy(v_sc[c][:], tab_sc[:].indirect(idx[:, list_cols(c)]))

        w1_bf = [held([P, PACK, P, PACK], BF16, f"w1_bf{a}") for a in range(PASSES)]
        w1_codes = [held([P, H], U32, f"w1_codes{a}") for a in range(PASSES)]
        w1_sc = [held([P, H], U8, f"w1_sc{a}") for a in range(PASSES)]

        def w1_views(a, lo, hi):
            return (
                w1_bf[a][:].rearrange("p t m j -> p m j t")[:, lo:hi],
                w1_raw[a][:].rearrange("p j (m t) -> p m j t", t=PACK)[:, lo:hi],
            )

        def quantize_w1(a):
            nc.vector.quantize_mx(
                out=w1_codes[a][:].bitcast(E4M3),
                scales=w1_sc[a][:],
                in_=w1_bf[a][:].rearrange("p t m j -> p (t m j)"),
            )

        w2_codes = held([P, PASSES, H], I32, "w2_codes")
        w2_sc = held([P, H], U8, "w2_sc")

        gather_words(0, 0)
        gather_scales(0)
        nc.scalar.copy(*w1_views(0, 0, P))
        gather_words(0, 1)
        gather_scales(1)
        nc.vector.tensor_copy(
            w2_sc[:].rearrange("p (t m) -> p t m", t=PACK),
            w2_raw_sc[:].rearrange("p (m t) -> p t m", t=PACK),
        )
        nc.vector.tensor_copy(*w1_views(1, 0, P // 2))
        nc.scalar.copy(*w1_views(1, P // 2, P))
        quantize_w1(0)
        quantize_w1(1)
        gather_words(1, 0)
        nc.scalar.copy(
            w2_codes[:].bitcast(U32).rearrange("p a (t m) -> p a m t", t=PACK),
            w2_raw[:].bitcast(U32).rearrange("p a (m t) -> p a m t", t=PACK),
        )
        gather_words(1, 1)

        look = [held([P, PACK, CHUNK], F32, f"look{c}") for c in range(CHUNKS)]
        top = held([P, PACK], F32, "top")
        shift = held([P, PACK], F32, "shift")
        temp_neg = held([P, PACK], F32, "temp_neg")
        nc.scalar.activation(out=temp_neg[:], in_=temp_sb[:], func=ACT.Copy, scale=-1.0)

        for t in range(PACK):
            first_tile = t == 0
            r_cols = slice(t * P, (t + 1) * P)
            vec_col = slice(t, t + 1)
            h = keep.tile([P, S], F32, tag="h")
            bent = ring.tile([P, S], F32, tag="bent")
            linear = None if first_tile else ring.tile([P, S], F32, tag="linear", name="linear")
            for c in range(CHUNKS):
                bent_ps = psum.tile([P, CHUNK], F32, tag="function", bufs=FUNCTION_BANKS)
                linear_ps = psum.tile([P, CHUNK], F32, tag="plain")
                for a in range(PASSES):
                    nc.tensor.matmul_mx(
                        out=bent_ps[:],
                        lhsT=w1_codes[a][:, r_cols].bitcast(E4M3),
                        lhsT_scale=w1_sc[a][:, r_cols],
                        rhs=v_codes[a][c][:].bitcast(E4M3),
                        rhs_scale=v_sc[c][BLOCKS * a :, :],
                        start=(a == 0),
                        stop=(a == PASSES - 1),
                    )
                for a in range(PASSES):
                    nc.tensor.matmul_mx(
                        out=linear_ps[:],
                        lhsT=w2_codes[:, a, r_cols].bitcast(E4M3),
                        lhsT_scale=w2_sc[BLOCKS * a :, r_cols],
                        rhs=v_codes[a][c][:].bitcast(E4M3),
                        rhs_scale=v_sc[c][BLOCKS * a :, :],
                        start=(a == 0),
                        stop=(a == PASSES - 1),
                    )
                cols = chunk_cols(c)
                nc.scalar.activation(out=bent[:, cols], in_=bent_ps[:], func=ACT.Tanh)
                if first_tile:
                    nc.vector.tensor_scalar(
                        bent[:, cols], bent[:, cols], gain1_sb[:, vec_col], b2_sb[:, vec_col], ALU.mult, ALU.add
                    )
                    nc.vector.tensor_tensor(h[:, cols], linear_ps[:], bent[:, cols], ALU.add)
                    nc.vector.tensor_tensor(
                        page[t][:].indirect(idx2[:, list_cols(c)]), h[:, cols], wg[:, cols], ALU.mult
                    )
                else:
                    nc.scalar.activation(
                        out=bent[:, cols], in_=bent[:, cols], func=ACT.Identity,
                        scale=gain1_sb[:, vec_col], bias=b2_sb[:, vec_col],
                    )
                    nc.scalar.copy(linear[:, cols], linear_ps[:])
            if not first_tile:
                nc.gpsimd.tensor_tensor(h[:], linear[:], bent[:], ALU.add)
                nc.vector.tensor_tensor(page[t][:].indirect(idx2[:]), h[:], wg[:, t * S : (t + 1) * S], ALU.mult)
            nc.vector.reduce_max(top[:, vec_col], page[t][:], AXIS.X)
            nc.scalar.activation(
                out=shift[:, vec_col], in_=top[:, vec_col], func=ACT.Copy, scale=temp_neg[:, vec_col]
            )
            for c in range(CHUNKS):
                nc.scalar.activation(
                    out=look[c][:, t, :],
                    in_=page[t][:].indirect(idx3[:, list_cols(c)]),
                    func=ACT.Exp,
                    bias=shift[:, vec_col],
                    scale=temp_sb[:, vec_col],
                )

        w3_bf = held([P, N, PACK], BF16, "w3_bf")
        w3_codes = held([P, N], U32, "w3_codes")
        w3_sc = held([P, N], U8, "w3_sc")
        nc.scalar.copy(
            w3_bf[:].rearrange("p (g i) j -> p g j i", i=LINE),
            w3_raw[:].rearrange("p j (g i) -> p g j i", i=LINE),
        )
        nc.vector.quantize_mx(
            out=w3_codes[:].bitcast(E4M3), scales=w3_sc[:], in_=w3_bf[:].rearrange("p n j -> p (n j)")
        )
        one = held([P, 1], F32, "one")
        phase = held([P, 1], F32, "phase")
        gain2_m2 = held([P, OUT_TILES], F32, "gain2_m2")
        nc.gpsimd.memset(one[:], 1.0)
        nc.gpsimd.tensor_scalar(phase[:], one[:], -math.pi / 4, 0.0, ALU.mult, ALU.add)
        nc.scalar.activation(out=gain2_m2[:], in_=gain2_sb[:], func=ACT.Copy, scale=-2.0)

        x_codes, x_sc = [], []
        for c in range(CHUNKS):
            x_bf = keep.tile([P, CHUNK, PACK], BF16, tag="x_bf", align_bytes=64)
            nc.vector.tensor_tensor(
                x_bf[:].rearrange("p (g i) t -> p g t i", i=LINE),
                look[c][:].rearrange("p t (g i) -> p g t i", i=LINE),
                mix_sb[:, :, chunk_cols(c)].rearrange("p t (g i) -> p g t i", i=LINE),
                ALU.mult,
            )
            x_codes.append(held([P, CHUNK], U32, f"x_codes{c}"))
            x_sc.append(held([P, CHUNK], U8, f"x_sc{c}"))
            nc.vector.quantize_mx(
                out=x_codes[c][:].bitcast(E4M3), scales=x_sc[c][:], in_=x_bf[:].rearrange("p m t -> p (m t)")
            )

        for c in range(CHUNKS):
            for u in range(OUT_TILES):
                n_cols = slice(u * P, (u + 1) * P)
                gain_col = slice(u, u + 1)
                wave_ps = psum.tile([P, CHUNK], F32, tag="function", bufs=FUNCTION_BANKS)
                plain_ps = psum.tile([P, CHUNK], F32, tag="plain")
                nc.tensor.matmul_mx(
                    out=wave_ps[:],
                    lhsT=w3_codes[:, n_cols].bitcast(E4M3),
                    lhsT_scale=w3_sc[:, n_cols],
                    rhs=x_codes[c][:].bitcast(E4M3),
                    rhs_scale=x_sc[c][:],
                    start=True,
                    stop=True,
                )
                nc.tensor.matmul_mx(
                    out=plain_ps[:],
                    lhsT=w4_codes[:, 2 * u * P : 2 * (u + 1) * P].bitcast(E2M1),
                    lhsT_scale=w4_sc[:, n_cols],
                    rhs=x_codes[c][:].bitcast(E4M3),
                    rhs_scale=x_sc[c][:],
                    start=True,
                    stop=True,
                )
                score = tail.tile([P, CHUNK], F32, tag="score")
                nc.scalar.activation(out=score[:], in_=wave_ps[:], func=ACT.Sin, scale=0.5, bias=phase[:])
                nc.scalar.activation(out=score[:], in_=score[:], func=ACT.Square)
                nc.vector.scalar_tensor_tensor(
                    score[:], score[:], gain2_m2[:, gain_col], plain_ps[:], ALU.mult, ALU.add
                )
                nc.vector.scalar_tensor_tensor(
                    score[:], score[:], gain2_sb[:, gain_col], prior_sb[:, u, chunk_cols(c)], ALU.add, ALU.add
                )
                nc.sync.dma_start(out=out[n_cols, chunk_cols(c)], in_=score[:])
